import numpy as np
import ml_dtypes

BF16 = ml_dtypes.bfloat16


def bf(x):
    return np.asarray(x, np.float32).astype(BF16)


def f32(x):
    return np.asarray(x, np.float32)


def f64(x):
    return np.asarray(x).astype(np.float64)


def striped(idx):
    return np.tile(idx.reshape(-1, 16).T, (8, 1))


S, K, M, N, D, V = 1024, 256, 128, 512, 4, 128


def setup_inputs():
    return {"table": bf(np.random.standard_normal((K, S))), "w": bf(np.random.standard_normal((K, M)) / np.sqrt(D * K)), "s": f32(0.5 + np.random.random_sample((M, 1))), "b": f32(0.5 * np.random.standard_normal((M, 1))), "offs": striped(np.random.permutation(np.tile(np.arange(S), 2))[:N])}


def reference(table, w, s, b, offs):
    idx = offs[:16].T.reshape(-1)
    x = f64(table)[:, idx]
    y = f64(w).T @ sum(x[:, t * V : (t + 1) * V] for t in range(D))
    return y * f64(s) + f64(b)

@@ -1,0 +1,53 @@
+import concourse.mybir as mybir
+
+BF16, F32, U16 = mybir.dt.bfloat16, mybir.dt.float32, mybir.dt.uint16
+MULT, ADD = mybir.AluOpType.mult, mybir.AluOpType.add
+
+P = 128
+K = 256
+S = 1024
+M = 128
+V = 128
+D = 4
+BLOCKS = K // P
+PIECE_COLS = V // 16
+
+FLOPS = 2 * K * M * V + (D - 1) * K * V + 2 * M * V
+
+
+def tile_gather_matmul_kernel(tc, table, w, s, b, offs, out):
+    nc = tc.nc
+    with (
+        tc.tile_pool(name="held", bufs=1) as held,
+        tc.psum_pool(name="psum", bufs=1) as psum,
+    ):
+        offsets = held.tile([P, D * PIECE_COLS], U16, name="offsets")
+        nc.sync.dma_start(offsets[:], offs)
+
+        weights = held.tile([P, BLOCKS, M], BF16, name="weights")
+        nc.scalar.dma_start(weights[:], w.rearrange("(a p) m -> p a m", p=P))
+
+        windows = [held.tile([P, S], BF16, name="window%d" % a) for a in range(BLOCKS)]
+        nc.sync.dma_start(windows[0][:], table[0:P, :])
+        nc.scalar.dma_start(windows[1][:], table[P : 2 * P, :])
+
+        gain = held.tile([P, 1], F32, name="gain")
+        shift = held.tile([P, 1], F32, name="shift")
+        nc.gpsimd.dma_start(gain[:], s)
+        nc.gpsimd.dma_start(shift[:], b)
+
+        y = psum.tile([M, V], F32, name="y")
+        steps = [(a, t) for a in range(BLOCKS) for t in range(D)]
+        for i, (a, t) in enumerate(steps):
+            piece = offsets[:, t * PIECE_COLS : (t + 1) * PIECE_COLS]
+            nc.tensor.matmul(
+                y[:],
+                weights[:, a, :],
+                windows[a][:].indirect(piece),
+                start=(i == 0),
+                stop=(i == len(steps) - 1),
+            )
+
+        result = held.tile([M, V], F32, name="result")
+        nc.vector.tensor_scalar(result[:], y[:], gain[:], shift[:], MULT, ADD)
+        nc.sync.dma_start(out, result[:])

@@ -28,13 +28,13 @@ def tile_gather_matmul_kernel(tc, table, w, s, b, offs, out):
         nc.scalar.dma_start(weights[:], w.rearrange("(a p) m -> p a m", p=P))
 
         windows = [held.tile([P, S], BF16, name="window%d" % a) for a in range(BLOCKS)]
-        nc.sync.dma_start(windows[0][:], table[0:P, :])
-        nc.scalar.dma_start(windows[1][:], table[P : 2 * P, :])
+        for a in range(BLOCKS):
+            nc.sync.dma_start(windows[a][:], table[a * P : (a + 1) * P, :])
 
         gain = held.tile([P, 1], F32, name="gain")
         shift = held.tile([P, 1], F32, name="shift")
-        nc.gpsimd.dma_start(gain[:], s)
-        nc.gpsimd.dma_start(shift[:], b)
+        nc.scalar.dma_start(gain[:], s)
+        nc.scalar.dma_start(shift[:], b)
 
         y = psum.tile([M, V], F32, name="y")
         steps = [(a, t) for a in range(BLOCKS) for t in range(D)]

@@ -10,6 +10,8 @@ M = 128
 V = 128
 D = 4
 BLOCKS = K // P
+WARM_COLS = 256
+WARM_UPS = 5
 PIECE_COLS = V // 16
 
 FLOPS = 2 * K * M * V + (D - 1) * K * V + 2 * M * V
@@ -35,6 +37,12 @@ def tile_gather_matmul_kernel(tc, table, w, s, b, offs, out):
         shift = held.tile([P, 1], F32, name="shift")
         nc.scalar.dma_start(gain[:], s)
         nc.scalar.dma_start(shift[:], b)
+
+        zeros = held.tile([P, WARM_COLS], BF16, name="zeros")
+        nc.vector.memset(zeros[:], 0.0)
+        unread = psum.tile([P, WARM_COLS], F32, name="unread")
+        for i in range(WARM_UPS):
+            nc.tensor.matmul(unread[:], zeros[:, 0:P], zeros[:], start=True, stop=True)
 
         y = psum.tile([M, V], F32, name="y")
         steps = [(a, t) for a in range(BLOCKS) for t in range(D)]

@@ -57,5 +57,7 @@ def tile_gather_matmul_kernel(tc, table, w, s, b, offs, out):
             )
 
         result = held.tile([M, V], F32, name="result")
-        nc.vector.tensor_scalar(result[:], y[:], gain[:], shift[:], MULT, ADD)
-        nc.sync.dma_start(out, result[:])
+        for h, queue in enumerate((nc.sync, nc.scalar)):
+            cols = slice(h * V // 2, (h + 1) * V // 2)
+            nc.vector.tensor_scalar(result[:, cols], y[:, cols], gain[:], shift[:], MULT, ADD)
+            queue.dma_start(out[:, cols], result[:, cols])

@@ -11,7 +11,7 @@ V = 128
 D = 4
 BLOCKS = K // P
 WARM_COLS = 256
-WARM_UPS = 5
+WARM_UPS = 8
 PIECE_COLS = V // 16
 
 FLOPS = 2 * K * M * V + (D - 1) * K * V + 2 * M * V

import concourse.mybir as mybir

BF16, F32, U16 = mybir.dt.bfloat16, mybir.dt.float32, mybir.dt.uint16
MULT, ADD = mybir.AluOpType.mult, mybir.AluOpType.add

P = 128
K = 256
S = 1024
M = 128
V = 128
D = 4
BLOCKS = K // P
WARM_COLS = 256
WARM_UPS = 8
PIECE_COLS = V // 16

FLOPS = 2 * K * M * V + (D - 1) * K * V + 2 * M * V


def tile_gather_matmul_kernel(tc, table, w, s, b, offs, out):
    nc = tc.nc
    with (
        tc.tile_pool(name="held", bufs=1) as held,
        tc.psum_pool(name="psum", bufs=1) as psum,
    ):
        offsets = held.tile([P, D * PIECE_COLS], U16, name="offsets")
        nc.sync.dma_start(offsets[:], offs)

        weights = held.tile([P, BLOCKS, M], BF16, name="weights")
        nc.scalar.dma_start(weights[:], w.rearrange("(a p) m -> p a m", p=P))

        windows = [held.tile([P, S], BF16, name="window%d" % a) for a in range(BLOCKS)]
        for a in range(BLOCKS):
            nc.sync.dma_start(windows[a][:], table[a * P : (a + 1) * P, :])

        gain = held.tile([P, 1], F32, name="gain")
        shift = held.tile([P, 1], F32, name="shift")
        nc.scalar.dma_start(gain[:], s)
        nc.scalar.dma_start(shift[:], b)

        zeros = held.tile([P, WARM_COLS], BF16, name="zeros")
        nc.vector.memset(zeros[:], 0.0)
        unread = psum.tile([P, WARM_COLS], F32, name="unread")
        for i in range(WARM_UPS):
            nc.tensor.matmul(unread[:], zeros[:, 0:P], zeros[:], start=True, stop=True)

        y = psum.tile([M, V], F32, name="y")
        steps = [(a, t) for a in range(BLOCKS) for t in range(D)]
        for i, (a, t) in enumerate(steps):
            piece = offsets[:, t * PIECE_COLS : (t + 1) * PIECE_COLS]
            nc.tensor.matmul(
                y[:],
                weights[:, a, :],
                windows[a][:].indirect(piece),
                start=(i == 0),
                stop=(i == len(steps) - 1),
            )

        result = held.tile([M, V], F32, name="result")
        for h, queue in enumerate((nc.sync, nc.scalar)):
            cols = slice(h * V // 2, (h + 1) * V // 2)
            nc.vector.tensor_scalar(result[:, cols], y[:, cols], gain[:], shift[:], MULT, ADD)
            queue.dma_start(out[:, cols], result[:, cols])
